import numpy as np
import ml_dtypes


def mxq(x, axis, fmt="e4m3"):
    dtype, down = {"e4m3": (ml_dtypes.float8_e4m3fn, 7), "e5m2": (ml_dtypes.float8_e5m2, 14)}[fmt]
    v = np.moveaxis(np.asarray(x, np.float32).astype(ml_dtypes.bfloat16).astype(np.float64), axis, -1)
    blocks = v.reshape(v.shape[:-1] + (-1, 32))
    amax = np.abs(blocks).max(-1, keepdims=True)
    byte = np.maximum(np.where(amax > 0, np.frexp(amax)[1] - 1 + 127, 0) - down, 1)
    scale = np.exp2(byte - 127.0)
    codes = (blocks / scale).astype(np.float32).astype(dtype).astype(np.float64)
    return np.moveaxis((codes * scale).reshape(v.shape), -1, axis)


WIDE = False


def mx_kscale(k):
    if not WIDE:
        return np.ones(k)
    levels = np.array([10, -10, 5, -5, 0])
    if k % 512:
        return np.exp2(np.random.permutation(np.resize(levels, k // 32))).repeat(32)
    a = np.empty((k // 512, 16))
    for p in range(k // 512):
        a[p, :8] = np.random.permutation(np.resize(levels, 8))
        for g in range(8):
            far = levels[np.abs(levels - a[p, g]) >= 10]
            a[p, g + 8] = far[np.random.randint(len(far))]
    return np.exp2(a.ravel()).repeat(32)


def f64(x):
    return np.asarray(x).astype(np.float64)


def striped(idx):
    return np.tile(idx.reshape(-1, 16).T, (8, 1)).astype(np.uint16)


def unstriped(offs):
    return offs[:16].T.reshape(-1).astype(np.int64)

def planes(y):
    n, m = y.shape
    v = y.astype(np.float32).astype(ml_dtypes.bfloat16).astype(np.float64).reshape(n // 32, 32, m)
    top = np.abs(v).max(1)
    byte = np.clip(np.where(top > 0, np.frexp(top)[1] - 1 + 127 - 7, 1), 1, 254)
    codes = (v * np.exp2(127.0 - byte)[:, None, :]).reshape(n, m).astype(np.float32).astype(ml_dtypes.float8_e4m3fn).view(np.uint8)
    words = codes.reshape(n // 512, 128, 4, m).transpose(0, 1, 3, 2)
    return np.ascontiguousarray(words), np.ascontiguousarray(byte.astype(np.uint8).reshape(n // 512, 16, m))


K, T, S, H = 512, 1024, 512, 512


def setup_inputs():
    n = np.random.standard_normal
    s = mx_kscale(K)[:, None]
    u = mx_kscale(H)
    return {
        "xT": (n((K, T)) * s).astype(np.float32),
        "w1": (n((K, H)) / np.sqrt(K) / s).astype(np.float32),
        "w2": (n((H, H)) / np.sqrt(H) / u[:, None]).astype(np.float32),
        "gamma": (np.random.uniform(0.5, 1.5, (H, 1)) * u[:, None]).astype(np.float32),
        "offs": striped(np.random.permutation(T)[:S]),
    }


def reference(xT, w1, w2, gamma, offs):
    xq = mxq(f64(xT)[:, unstriped(offs)], 0, "e4m3")
    h = mxq(f64(w1), 0, "e4m3").T @ xq
    hn = (h - h.mean(axis=1, keepdims=True)) / np.sqrt(h.var(axis=1, keepdims=True) + 1e-5)
    z = f64(gamma) * hn
    out_0 = mxq(f64(w2), 0, "e4m3").T @ mxq(z, 0, "e4m3")
    return (out_0,) + planes(out_0)

@@ -1,0 +1,187 @@
+from contextlib import ExitStack
+
+import concourse.mybir as mybir
+
+K, T, S, H = 512, 1024, 512, 512
+FLOPS = 2 * K * H * S + 2 * H * H * S
+
+F32 = mybir.dt.float32
+BF16 = mybir.dt.bfloat16
+I32 = mybir.dt.int32
+U32 = mybir.dt.uint32
+U16 = mybir.dt.uint16
+U8 = mybir.dt.uint8
+FP8X4 = mybir.dt.float8_e4m3fn_x4
+ACT = mybir.ActivationFunctionType
+ALU = mybir.AluOpType
+
+P = 128
+PACK = 4
+EPS = 1e-5
+XV = 352
+CH = 128
+NCH = S // CH
+HALF = H // 2
+
+
+def tile_picked_inorm_none_lo_kernel(tc, xT, w1, w2, gamma, offs, out_0, out_1, out_2):
+    nc = tc.nc
+
+    def gp_copy(out, in_):
+        nc.gpsimd.tensor_scalar(out=out, in0=in_, scalar1=1.0, scalar2=0.0, op0=ALU.mult, op1=ALU.add)
+
+    def interleave(copy, dst, src):
+        copy(out=dst.rearrange("p (c i) t -> p c t i", i=4), in_=src.rearrange("p t (c i) -> p c t i", i=4))
+
+    def deal(copy, dst, raw, half, lo, hi):
+        m0 = half * (HALF // PACK)
+        copy(out=dst[:, :, m0 + lo : m0 + hi, :].rearrange("p t m j -> p m j t"),
+             in_=raw[:, :, PACK * lo : PACK * hi].rearrange("p j (m t) -> p m j t", t=PACK))
+
+    with ExitStack() as ctx:
+        keep = ctx.enter_context(tc.tile_pool(name="keep", bufs=1))
+        psum = ctx.enter_context(tc.psum_pool(name="psum", bufs=1))
+
+        offsets = keep.tile([P, S // 16], U16, name="offsets")
+        x_rows = xT.rearrange("(p j) n -> j p n", j=PACK)
+        x_raw = [keep.tile([P, T], F32, name=f"x_raw{j}") for j in range(PACK)]
+        w1_raw = [keep.tile([P, PACK, HALF], F32, name=f"w1_raw{h}") for h in range(2)]
+        w2_raw = [keep.tile([P, PACK, HALF], F32, name=f"w2_raw{h}") for h in range(2)]
+        gam = keep.tile([P, PACK], F32, name="gam")
+        nc.scalar.dma_start(out=gam[:], in_=gamma.rearrange("(p t) o -> p (t o)", t=PACK))
+        nc.sync.dma_start(out=x_raw[0][:], in_=x_rows[0])
+        nc.sync.dma_start(offsets[:], offs)
+        for j in range(1, PACK):
+            nc.sync.dma_start(out=x_raw[j][:], in_=x_rows[j])
+        for raw, w in ((w1_raw, w1), (w2_raw, w2)):
+            rows = w.rearrange("(p j) n -> p j n", j=PACK)
+            for h in range(2):
+                nc.sync.dma_start(out=raw[h][:], in_=rows[:, :, h * HALF : (h + 1) * HALF])
+
+        factors = keep.tile([P, PACK, 2], F32, name="factors")
+        neg_gam = keep.tile([P, PACK], F32, name="neg_gam")
+        nc.vector.tensor_copy(out=factors[:, :, 0], in_=gam[:])
+        nc.vector.tensor_scalar(out=neg_gam[:], in0=gam[:], scalar1=-1.0, scalar2=None, op0=ALU.mult)
+
+        x_il = keep.tile([P, S, PACK], BF16, name="x_il", align_bytes=64)
+        xg_s = keep.tile([P, PACK, S - XV], BF16, name="xg_s")
+        for j in range(PACK):
+            nc.vector.tensor_copy(out=x_il[:, :XV, j], in_=x_raw[j][:].indirect(offsets[:, : XV // 16]))
+            nc.scalar.activation(out=xg_s[:, j, :], in_=x_raw[j][:].indirect(offsets[:, XV // 16 :]), func=ACT.Copy)
+        interleave(nc.scalar.copy, x_il[:, XV:, :], xg_s[:])
+        x_codes = keep.tile([P, S], U32, name="x_codes", align_bytes=64)
+        x_scales = keep.tile([P, S], U8, name="x_scales", align_bytes=64)
+        for h in range(2):
+            cols = slice(h * (S // 2), (h + 1) * (S // 2))
+            nc.vector.quantize_mx(out=x_codes[:, cols].bitcast(FP8X4), scales=x_scales[:, cols],
+                                  in_=x_il[:, cols, :].rearrange("p c t -> p (c t)"))
+
+        w1_il = keep.tile([P, PACK, P, PACK], BF16, name="w1_il", align_bytes=64)
+        deal(nc.vector.tensor_copy, w1_il, w1_raw[0], 0, 0, 24)
+        deal(nc.scalar.copy, w1_il, w1_raw[0], 0, 24, 64)
+        deal(nc.vector.tensor_copy, w1_il, w1_raw[1], 1, 0, 44)
+        deal(nc.scalar.copy, w1_il, w1_raw[1], 1, 44, 64)
+        w1_codes = [keep.tile([P, P], U32, name=f"w1_codes{t}", align_bytes=64) for t in range(PACK)]
+        w1_scales = [keep.tile([P, P], U8, name=f"w1_scales{t}", align_bytes=64) for t in range(PACK)]
+        for t in range(PACK):
+            nc.vector.quantize_mx(out=w1_codes[t][:].bitcast(FP8X4), scales=w1_scales[t][:],
+                                  in_=w1_il[:, t, :, :].rearrange("p m j -> p (m j)"))
+
+        h_ps = [psum.tile([P, S], F32, name=f"h_ps{t}", tag=f"h_ps{t}") for t in range(PACK)]
+        for t in range(PACK):
+            nc.tensor.matmul_mx(out=h_ps[t][:], lhsT=w1_codes[t][:].bitcast(FP8X4), lhsT_scale=w1_scales[t][:],
+                                rhs=x_codes[:].bitcast(FP8X4), rhs_scale=x_scales[:], start=True, stop=True)
+
+        w2_il = keep.tile([P, PACK, P, PACK], BF16, name="w2_il", align_bytes=64)
+        for t in range(PACK):
+            gp_copy(w2_il[:, t, 64 : 128, :], w2_raw[1][:].rearrange("p j (m t) -> p t m j", t=PACK)[:, t, :, :])
+
+        deal(nc.scalar.copy, w2_il, w2_raw[0], 0, 32, 64)
+        on_vector = (9,)
+        in_halves = (2, 3,)
+        z_pl = keep.tile([P, NCH, PACK, CH], BF16, name="z_pl")
+        mv = [keep.tile([P, 2], F32, name=f"mv{t}") for t in range(PACK)]
+        sb = [keep.tile([P, 2], F32, name=f"sb{t}") for t in range(PACK)]
+        for t in range(PACK):
+            stats = keep.tile([P, 6], F32, name=f"stats{t}")
+            rstd = keep.tile([P, 1], F32, name=f"rstd{t}")
+            nc.vector.bn_stats(out=stats[:], in_=h_ps[t][:])
+            nc.vector.bn_aggr(out=mv[t][:], in_=stats[:])
+            nc.scalar.activation(out=rstd[:], in_=mv[t][:, 1:2], func=ACT.Abs_reciprocal_sqrt, bias=EPS)
+            if t in on_vector:
+                nc.scalar.activation(out=sb[t][:, 0:1], in_=gam[:, t : t + 1], func=ACT.Copy, scale=rstd[:])
+            else:
+                nc.scalar.activation(out=factors[:, t, 1:2], in_=mv[t][:, 0:1], func=ACT.Copy, scale=neg_gam[:, t : t + 1])
+                nc.scalar.activation(out=sb[t][:], in_=factors[:, t, :], func=ACT.Copy, scale=rstd[:])
+        deal(nc.vector.tensor_copy, w2_il, w2_raw[0], 0, 0, 32)
+
+        w2_codes = keep.tile([P, H], U32, name="w2_codes", align_bytes=64)
+        w2_scales = keep.tile([P, H], U8, name="w2_scales", align_bytes=64)
+        for t in range(PACK):
+            cols = slice(t * P, (t + 1) * P)
+            nc.vector.quantize_mx(out=w2_codes[:, cols].bitcast(FP8X4), scales=w2_scales[:, cols],
+                                  in_=w2_il[:, t, :, :].rearrange("p m j -> p (m j)"))
+
+        def normalise(t, c0, c1):
+            src = h_ps[t][:, c0 * CH : c1 * CH].rearrange("p (c n) -> p c n", n=CH)
+            if t in on_vector:
+                nc.vector.tensor_scalar(out=z_pl[:, c0:c1, t, :], in0=src, scalar1=mv[t][:, 0:1], scalar2=sb[t][:, 0:1],
+                                        op0=ALU.subtract, op1=ALU.mult)
+            else:
+                nc.scalar.activation(out=z_pl[:, c0:c1, t, :], in_=src, func=ACT.Identity,
+                                     scale=sb[t][:, 0:1], bias=sb[t][:, 1:2])
+
+        for t in range(PACK):
+            normalise(t, 0, 1 if t in in_halves else NCH)
+
+        out_rows = out_0.rearrange("(p t) n -> p t n", t=PACK)
+        words_hbm = out_1.rearrange("z p c r -> p (z c r)").bitcast(I32)
+        scales_hbm = out_2.rearrange("z q c -> (z q) c").bitcast(I32)
+        o_scales = keep.tile([P, S], U8, name="o_scales", align_bytes=64)
+        o_words = keep.tile([P, S], U32, name="o_words", align_bytes=64)
+        z_copy = [nc.vector.tensor_copy, nc.vector.tensor_copy, nc.vector.tensor_copy, nc.vector.tensor_copy]
+        o_copy = [nc.vector.tensor_copy, nc.vector.tensor_copy, nc.scalar.copy, nc.vector.tensor_copy]
+        e_copy = [nc.scalar.copy, nc.scalar.copy, nc.scalar.copy, nc.scalar.copy]
+        tail = "AABC"
+        o_ps = []
+        for c in range(NCH):
+            z_il = keep.tile([P, CH, PACK], BF16, name=f"z_il{c}", align_bytes=64)
+            z_codes = keep.tile([P, CH], U32, name=f"z_codes{c}", align_bytes=64)
+            z_scales = keep.tile([P, CH], U8, name=f"z_scales{c}", align_bytes=64)
+            if c == 1:
+                for t in in_halves:
+                    normalise(t, 1, NCH)
+            interleave(z_copy[c], z_il[:], z_pl[:, c, :, :])
+            nc.vector.quantize_mx(out=z_codes[:].bitcast(FP8X4), scales=z_scales[:],
+                                  in_=z_il[:].rearrange("p c t -> p (c t)"))
+            if c < NCH - 1:
+                bank = psum.tile([P, PACK, CH], F32, name=f"o_ps{c}")
+                parts = [bank[:, t, :] for t in range(PACK)]
+                o_ps.append(bank)
+            else:
+                last = [psum.tile([P, 2, CH], F32, name="o_last0"), psum.tile([P, 2, CH], F32, name="o_last1", tag="h_ps0")]
+                parts = [last[t // 2][:, t % 2, :] for t in range(PACK)]
+            for t in range(PACK):
+                cols = slice(t * P, (t + 1) * P)
+                nc.tensor.matmul_mx(out=parts[t], lhsT=w2_codes[:, cols].bitcast(FP8X4), lhsT_scale=w2_scales[:, cols],
+                                    rhs=z_codes[:].bitcast(FP8X4), rhs_scale=z_scales[:], start=True, stop=True)
+        for c in range(NCH):
+            cols = slice(c * CH, (c + 1) * CH)
+            o_f32 = keep.tile([P, PACK, CH], F32, name=f"o_f32{c}")
+            o_il = keep.tile([P, CH, PACK], BF16, name=f"o_il{c}", align_bytes=64)
+            if c < NCH - 1:
+                nc.scalar.copy(out=o_f32[:], in_=o_ps[c][:])
+                nc.sync.dma_start(out=out_rows[:, :, cols], in_=o_f32[:])
+            else:
+                for u, copy in enumerate((nc.scalar.copy, nc.vector.tensor_copy)):
+                    copy(out=o_f32[:, 2 * u : 2 * u + 2, :], in_=last[u][:])
+                nc.sync.dma_start(out=out_rows[:, :, cols], in_=o_f32[:])
+            interleave(o_copy[c], o_il[:], o_f32[:])
+            nc.vector.quantize_mx(out=o_words[:, cols].bitcast(FP8X4), scales=o_scales[:, cols],
+                                  in_=o_il[:].rearrange("p c t -> p (c t)"))
+            if c >= NCH - 2:
+                done = slice(0, (NCH - 1) * CH) if c == NCH - 2 else cols
+                nc.sync.dma_start(out=words_hbm[:, done], in_=o_words[:, done].bitcast(I32))
+        for q in range(4):
+            queue = nc.sync if q % 2 == 0 else nc.scalar
+            queue.dma_start(out=scales_hbm[4 * q : 4 * q + 4, :], in_=o_scales[32 * q : 32 * q + 4, :].bitcast(I32))

@@ -35,8 +35,8 @@ def tile_picked_inorm_none_lo_kernel(tc, xT, w1, w2, gamma, offs, out_0, out_1, 
 
     def deal(copy, dst, raw, half, lo, hi):
         m0 = half * (HALF // PACK)
-        copy(out=dst[:, :, m0 + lo : m0 + hi, :].rearrange("p t m j -> p m j t"),
-             in_=raw[:, :, PACK * lo : PACK * hi].rearrange("p j (m t) -> p m j t", t=PACK))
+        copy(out=dst[:, :, m0 + lo : m0 + hi, :].rearrange("p t m j -> p m t j"),
+             in_=raw[:, :, PACK * lo : PACK * hi].rearrange("p j (m t) -> p m t j", t=PACK))
 
     with ExitStack() as ctx:
         keep = ctx.enter_context(tc.tile_pool(name="keep", bufs=1))

@@ -58,6 +58,9 @@ def tile_picked_inorm_none_lo_kernel(tc, xT, w1, w2, gamma, offs, out_0, out_1, 
             for h in range(2):
                 nc.sync.dma_start(out=raw[h][:], in_=rows[:, :, h * HALF : (h + 1) * HALF])
 
+        warm = keep.tile([P, 16], F32, name="warm")
+        nc.vector.memset(warm[:, 0:1], 1.0)
+        nc.scalar.activation(out=warm[:, 8:9], in_=warm[:, 0:1], func=ACT.Abs_reciprocal_sqrt)
         factors = keep.tile([P, PACK, 2], F32, name="factors")
         neg_gam = keep.tile([P, PACK], F32, name="neg_gam")
         nc.vector.tensor_copy(out=factors[:, :, 0], in_=gam[:])

@@ -18,7 +18,7 @@ ALU = mybir.AluOpType
 P = 128
 PACK = 4
 EPS = 1e-5
-XV = 352
+XV = 320
 CH = 128
 NCH = S // CH
 HALF = H // 2
@@ -26,9 +26,6 @@ HALF = H // 2
 
 def tile_picked_inorm_none_lo_kernel(tc, xT, w1, w2, gamma, offs, out_0, out_1, out_2):
     nc = tc.nc
-
-    def gp_copy(out, in_):
-        nc.gpsimd.tensor_scalar(out=out, in0=in_, scalar1=1.0, scalar2=0.0, op0=ALU.mult, op1=ALU.add)
 
     def interleave(copy, dst, src):
         copy(out=dst.rearrange("p (c i) t -> p c t i", i=4), in_=src.rearrange("p t (c i) -> p c t i", i=4))
@@ -80,8 +77,8 @@ def tile_picked_inorm_none_lo_kernel(tc, xT, w1, w2, gamma, offs, out_0, out_1, 
                                   in_=x_il[:, cols, :].rearrange("p c t -> p (c t)"))
 
         w1_il = keep.tile([P, PACK, P, PACK], BF16, name="w1_il", align_bytes=64)
-        deal(nc.vector.tensor_copy, w1_il, w1_raw[0], 0, 0, 24)
-        deal(nc.scalar.copy, w1_il, w1_raw[0], 0, 24, 64)
+        deal(nc.vector.tensor_copy, w1_il, w1_raw[0], 0, 0, 40)
+        deal(nc.scalar.copy, w1_il, w1_raw[0], 0, 40, 64)
         deal(nc.vector.tensor_copy, w1_il, w1_raw[1], 1, 0, 44)
         deal(nc.scalar.copy, w1_il, w1_raw[1], 1, 44, 64)
         w1_codes = [keep.tile([P, P], U32, name=f"w1_codes{t}", align_bytes=64) for t in range(PACK)]
@@ -96,10 +93,9 @@ def tile_picked_inorm_none_lo_kernel(tc, xT, w1, w2, gamma, offs, out_0, out_1, 
                                 rhs=x_codes[:].bitcast(FP8X4), rhs_scale=x_scales[:], start=True, stop=True)
 
         w2_il = keep.tile([P, PACK, P, PACK], BF16, name="w2_il", align_bytes=64)
-        for t in range(PACK):
-            gp_copy(w2_il[:, t, 64 : 128, :], w2_raw[1][:].rearrange("p j (m t) -> p t m j", t=PACK)[:, t, :, :])
 
-        deal(nc.scalar.copy, w2_il, w2_raw[0], 0, 32, 64)
+        deal(nc.scalar.copy, w2_il, w2_raw[0], 0, 16, 64)
+        deal(nc.scalar.copy, w2_il, w2_raw[1], 1, 40, 64)
         on_vector = (9,)
         in_halves = (2, 3,)
         z_pl = keep.tile([P, NCH, PACK, CH], BF16, name="z_pl")
@@ -110,13 +106,20 @@ def tile_picked_inorm_none_lo_kernel(tc, xT, w1, w2, gamma, offs, out_0, out_1, 
             rstd = keep.tile([P, 1], F32, name=f"rstd{t}")
             nc.vector.bn_stats(out=stats[:], in_=h_ps[t][:])
             nc.vector.bn_aggr(out=mv[t][:], in_=stats[:])
+            if t == PACK - 1:
+                centred = keep.tile([P, CH], F32, name="centred")
+                nc.vector.tensor_scalar(out=centred[:], in0=h_ps[t][:, :CH], scalar1=mv[t][:, 0:1], scalar2=gam[:, t : t + 1],
+                                        op0=ALU.subtract, op1=ALU.mult)
             nc.scalar.activation(out=rstd[:], in_=mv[t][:, 1:2], func=ACT.Abs_reciprocal_sqrt, bias=EPS)
+            if t == PACK - 1:
+                nc.vector.tensor_scalar(out=z_pl[:, 0, t, :], in0=centred[:], scalar1=rstd[:], scalar2=None, op0=ALU.mult)
             if t in on_vector:
                 nc.scalar.activation(out=sb[t][:, 0:1], in_=gam[:, t : t + 1], func=ACT.Copy, scale=rstd[:])
             else:
                 nc.scalar.activation(out=factors[:, t, 1:2], in_=mv[t][:, 0:1], func=ACT.Copy, scale=neg_gam[:, t : t + 1])
                 nc.scalar.activation(out=sb[t][:], in_=factors[:, t, :], func=ACT.Copy, scale=rstd[:])
-        deal(nc.vector.tensor_copy, w2_il, w2_raw[0], 0, 0, 32)
+        deal(nc.vector.tensor_copy, w2_il, w2_raw[0], 0, 0, 16)
+        deal(nc.vector.tensor_copy, w2_il, w2_raw[1], 1, 0, 40)
 
         w2_codes = keep.tile([P, H], U32, name="w2_codes", align_bytes=64)
         w2_scales = keep.tile([P, H], U8, name="w2_scales", align_bytes=64)
@@ -134,15 +137,15 @@ def tile_picked_inorm_none_lo_kernel(tc, xT, w1, w2, gamma, offs, out_0, out_1, 
                 nc.scalar.activation(out=z_pl[:, c0:c1, t, :], in_=src, func=ACT.Identity,
                                      scale=sb[t][:, 0:1], bias=sb[t][:, 1:2])
 
-        for t in range(PACK):
-            normalise(t, 0, 1 if t in in_halves else NCH)
+        for t in range(PACK - 1):
+            normalise(t, 0, 1 if t in in_halves else 2)
 
         out_rows = out_0.rearrange("(p t) n -> p t n", t=PACK)
         words_hbm = out_1.rearrange("z p c r -> p (z c r)").bitcast(I32)
         scales_hbm = out_2.rearrange("z q c -> (z q) c").bitcast(I32)
         o_scales = keep.tile([P, S], U8, name="o_scales", align_bytes=64)
         o_words = keep.tile([P, S], U32, name="o_words", align_bytes=64)
-        z_copy = [nc.vector.tensor_copy, nc.vector.tensor_copy, nc.vector.tensor_copy, nc.vector.tensor_copy]
+        z_copy = [nc.vector.tensor_copy, nc.vector.tensor_copy, nc.vector.tensor_copy, nc.scalar.copy]
         o_copy = [nc.vector.tensor_copy, nc.vector.tensor_copy, nc.scalar.copy, nc.vector.tensor_copy]
         e_copy = [nc.scalar.copy, nc.scalar.copy, nc.scalar.copy, nc.scalar.copy]
         tail = "AABC"
@@ -153,7 +156,10 @@ def tile_picked_inorm_none_lo_kernel(tc, xT, w1, w2, gamma, offs, out_0, out_1, 
             z_scales = keep.tile([P, CH], U8, name=f"z_scales{c}", align_bytes=64)
             if c == 1:
                 for t in in_halves:
-                    normalise(t, 1, NCH)
+                    normalise(t, 1, 2)
+            if c == 2:
+                for t in range(PACK):
+                    normalise(t, 2, NCH)
             interleave(z_copy[c], z_il[:], z_pl[:, c, :, :])
             nc.vector.quantize_mx(out=z_codes[:].bitcast(FP8X4), scales=z_scales[:],
                                   in_=z_il[:].rearrange("p c t -> p (c t)"))

from contextlib import ExitStack

import concourse.mybir as mybir

K, T, S, H = 512, 1024, 512, 512
FLOPS = 2 * K * H * S + 2 * H * H * S

F32 = mybir.dt.float32
BF16 = mybir.dt.bfloat16
I32 = mybir.dt.int32
U32 = mybir.dt.uint32
U16 = mybir.dt.uint16
U8 = mybir.dt.uint8
FP8X4 = mybir.dt.float8_e4m3fn_x4
ACT = mybir.ActivationFunctionType
ALU = mybir.AluOpType

P = 128
PACK = 4
EPS = 1e-5
XV = 320
CH = 128
NCH = S // CH
HALF = H // 2


def tile_picked_inorm_none_lo_kernel(tc, xT, w1, w2, gamma, offs, out_0, out_1, out_2):
    nc = tc.nc

    def interleave(copy, dst, src):
        copy(out=dst.rearrange("p (c i) t -> p c t i", i=4), in_=src.rearrange("p t (c i) -> p c t i", i=4))

    def deal(copy, dst, raw, half, lo, hi):
        m0 = half * (HALF // PACK)
        copy(out=dst[:, :, m0 + lo : m0 + hi, :].rearrange("p t m j -> p m t j"),
             in_=raw[:, :, PACK * lo : PACK * hi].rearrange("p j (m t) -> p m t j", t=PACK))

    with ExitStack() as ctx:
        keep = ctx.enter_context(tc.tile_pool(name="keep", bufs=1))
        psum = ctx.enter_context(tc.psum_pool(name="psum", bufs=1))

        offsets = keep.tile([P, S // 16], U16, name="offsets")
        x_rows = xT.rearrange("(p j) n -> j p n", j=PACK)
        x_raw = [keep.tile([P, T], F32, name=f"x_raw{j}") for j in range(PACK)]
        w1_raw = [keep.tile([P, PACK, HALF], F32, name=f"w1_raw{h}") for h in range(2)]
        w2_raw = [keep.tile([P, PACK, HALF], F32, name=f"w2_raw{h}") for h in range(2)]
        gam = keep.tile([P, PACK], F32, name="gam")
        nc.scalar.dma_start(out=gam[:], in_=gamma.rearrange("(p t) o -> p (t o)", t=PACK))
        nc.sync.dma_start(out=x_raw[0][:], in_=x_rows[0])
        nc.sync.dma_start(offsets[:], offs)
        for j in range(1, PACK):
            nc.sync.dma_start(out=x_raw[j][:], in_=x_rows[j])
        for raw, w in ((w1_raw, w1), (w2_raw, w2)):
            rows = w.rearrange("(p j) n -> p j n", j=PACK)
            for h in range(2):
                nc.sync.dma_start(out=raw[h][:], in_=rows[:, :, h * HALF : (h + 1) * HALF])

        warm = keep.tile([P, 16], F32, name="warm")
        nc.vector.memset(warm[:, 0:1], 1.0)
        nc.scalar.activation(out=warm[:, 8:9], in_=warm[:, 0:1], func=ACT.Abs_reciprocal_sqrt)
        factors = keep.tile([P, PACK, 2], F32, name="factors")
        neg_gam = keep.tile([P, PACK], F32, name="neg_gam")
        nc.vector.tensor_copy(out=factors[:, :, 0], in_=gam[:])
        nc.vector.tensor_scalar(out=neg_gam[:], in0=gam[:], scalar1=-1.0, scalar2=None, op0=ALU.mult)

        x_il = keep.tile([P, S, PACK], BF16, name="x_il", align_bytes=64)
        xg_s = keep.tile([P, PACK, S - XV], BF16, name="xg_s")
        for j in range(PACK):
            nc.vector.tensor_copy(out=x_il[:, :XV, j], in_=x_raw[j][:].indirect(offsets[:, : XV // 16]))
            nc.scalar.activation(out=xg_s[:, j, :], in_=x_raw[j][:].indirect(offsets[:, XV // 16 :]), func=ACT.Copy)
        interleave(nc.scalar.copy, x_il[:, XV:, :], xg_s[:])
        x_codes = keep.tile([P, S], U32, name="x_codes", align_bytes=64)
        x_scales = keep.tile([P, S], U8, name="x_scales", align_bytes=64)
        for h in range(2):
            cols = slice(h * (S // 2), (h + 1) * (S // 2))
            nc.vector.quantize_mx(out=x_codes[:, cols].bitcast(FP8X4), scales=x_scales[:, cols],
                                  in_=x_il[:, cols, :].rearrange("p c t -> p (c t)"))

        w1_il = keep.tile([P, PACK, P, PACK], BF16, name="w1_il", align_bytes=64)
        deal(nc.vector.tensor_copy, w1_il, w1_raw[0], 0, 0, 40)
        deal(nc.scalar.copy, w1_il, w1_raw[0], 0, 40, 64)
        deal(nc.vector.tensor_copy, w1_il, w1_raw[1], 1, 0, 44)
        deal(nc.scalar.copy, w1_il, w1_raw[1], 1, 44, 64)
        w1_codes = [keep.tile([P, P], U32, name=f"w1_codes{t}", align_bytes=64) for t in range(PACK)]
        w1_scales = [keep.tile([P, P], U8, name=f"w1_scales{t}", align_bytes=64) for t in range(PACK)]
        for t in range(PACK):
            nc.vector.quantize_mx(out=w1_codes[t][:].bitcast(FP8X4), scales=w1_scales[t][:],
                                  in_=w1_il[:, t, :, :].rearrange("p m j -> p (m j)"))

        h_ps = [psum.tile([P, S], F32, name=f"h_ps{t}", tag=f"h_ps{t}") for t in range(PACK)]
        for t in range(PACK):
            nc.tensor.matmul_mx(out=h_ps[t][:], lhsT=w1_codes[t][:].bitcast(FP8X4), lhsT_scale=w1_scales[t][:],
                                rhs=x_codes[:].bitcast(FP8X4), rhs_scale=x_scales[:], start=True, stop=True)

        w2_il = keep.tile([P, PACK, P, PACK], BF16, name="w2_il", align_bytes=64)

        deal(nc.scalar.copy, w2_il, w2_raw[0], 0, 16, 64)
        deal(nc.scalar.copy, w2_il, w2_raw[1], 1, 40, 64)
        on_vector = (9,)
        in_halves = (2, 3,)
        z_pl = keep.tile([P, NCH, PACK, CH], BF16, name="z_pl")
        mv = [keep.tile([P, 2], F32, name=f"mv{t}") for t in range(PACK)]
        sb = [keep.tile([P, 2], F32, name=f"sb{t}") for t in range(PACK)]
        for t in range(PACK):
            stats = keep.tile([P, 6], F32, name=f"stats{t}")
            rstd = keep.tile([P, 1], F32, name=f"rstd{t}")
            nc.vector.bn_stats(out=stats[:], in_=h_ps[t][:])
            nc.vector.bn_aggr(out=mv[t][:], in_=stats[:])
            if t == PACK - 1:
                centred = keep.tile([P, CH], F32, name="centred")
                nc.vector.tensor_scalar(out=centred[:], in0=h_ps[t][:, :CH], scalar1=mv[t][:, 0:1], scalar2=gam[:, t : t + 1],
                                        op0=ALU.subtract, op1=ALU.mult)
            nc.scalar.activation(out=rstd[:], in_=mv[t][:, 1:2], func=ACT.Abs_reciprocal_sqrt, bias=EPS)
            if t == PACK - 1:
                nc.vector.tensor_scalar(out=z_pl[:, 0, t, :], in0=centred[:], scalar1=rstd[:], scalar2=None, op0=ALU.mult)
            if t in on_vector:
                nc.scalar.activation(out=sb[t][:, 0:1], in_=gam[:, t : t + 1], func=ACT.Copy, scale=rstd[:])
            else:
                nc.scalar.activation(out=factors[:, t, 1:2], in_=mv[t][:, 0:1], func=ACT.Copy, scale=neg_gam[:, t : t + 1])
                nc.scalar.activation(out=sb[t][:], in_=factors[:, t, :], func=ACT.Copy, scale=rstd[:])
        deal(nc.vector.tensor_copy, w2_il, w2_raw[0], 0, 0, 16)
        deal(nc.vector.tensor_copy, w2_il, w2_raw[1], 1, 0, 40)

        w2_codes = keep.tile([P, H], U32, name="w2_codes", align_bytes=64)
        w2_scales = keep.tile([P, H], U8, name="w2_scales", align_bytes=64)
        for t in range(PACK):
            cols = slice(t * P, (t + 1) * P)
            nc.vector.quantize_mx(out=w2_codes[:, cols].bitcast(FP8X4), scales=w2_scales[:, cols],
                                  in_=w2_il[:, t, :, :].rearrange("p m j -> p (m j)"))

        def normalise(t, c0, c1):
            src = h_ps[t][:, c0 * CH : c1 * CH].rearrange("p (c n) -> p c n", n=CH)
            if t in on_vector:
                nc.vector.tensor_scalar(out=z_pl[:, c0:c1, t, :], in0=src, scalar1=mv[t][:, 0:1], scalar2=sb[t][:, 0:1],
                                        op0=ALU.subtract, op1=ALU.mult)
            else:
                nc.scalar.activation(out=z_pl[:, c0:c1, t, :], in_=src, func=ACT.Identity,
                                     scale=sb[t][:, 0:1], bias=sb[t][:, 1:2])

        for t in range(PACK - 1):
            normalise(t, 0, 1 if t in in_halves else 2)

        out_rows = out_0.rearrange("(p t) n -> p t n", t=PACK)
        words_hbm = out_1.rearrange("z p c r -> p (z c r)").bitcast(I32)
        scales_hbm = out_2.rearrange("z q c -> (z q) c").bitcast(I32)
        o_scales = keep.tile([P, S], U8, name="o_scales", align_bytes=64)
        o_words = keep.tile([P, S], U32, name="o_words", align_bytes=64)
        z_copy = [nc.vector.tensor_copy, nc.vector.tensor_copy, nc.vector.tensor_copy, nc.scalar.copy]
        o_copy = [nc.vector.tensor_copy, nc.vector.tensor_copy, nc.scalar.copy, nc.vector.tensor_copy]
        e_copy = [nc.scalar.copy, nc.scalar.copy, nc.scalar.copy, nc.scalar.copy]
        tail = "AABC"
        o_ps = []
        for c in range(NCH):
            z_il = keep.tile([P, CH, PACK], BF16, name=f"z_il{c}", align_bytes=64)
            z_codes = keep.tile([P, CH], U32, name=f"z_codes{c}", align_bytes=64)
            z_scales = keep.tile([P, CH], U8, name=f"z_scales{c}", align_bytes=64)
            if c == 1:
                for t in in_halves:
                    normalise(t, 1, 2)
            if c == 2:
                for t in range(PACK):
                    normalise(t, 2, NCH)
            interleave(z_copy[c], z_il[:], z_pl[:, c, :, :])
            nc.vector.quantize_mx(out=z_codes[:].bitcast(FP8X4), scales=z_scales[:],
                                  in_=z_il[:].rearrange("p c t -> p (c t)"))
            if c < NCH - 1:
                bank = psum.tile([P, PACK, CH], F32, name=f"o_ps{c}")
                parts = [bank[:, t, :] for t in range(PACK)]
                o_ps.append(bank)
            else:
                last = [psum.tile([P, 2, CH], F32, name="o_last0"), psum.tile([P, 2, CH], F32, name="o_last1", tag="h_ps0")]
                parts = [last[t // 2][:, t % 2, :] for t in range(PACK)]
            for t in range(PACK):
                cols = slice(t * P, (t + 1) * P)
                nc.tensor.matmul_mx(out=parts[t], lhsT=w2_codes[:, cols].bitcast(FP8X4), lhsT_scale=w2_scales[:, cols],
                                    rhs=z_codes[:].bitcast(FP8X4), rhs_scale=z_scales[:], start=True, stop=True)
        for c in range(NCH):
            cols = slice(c * CH, (c + 1) * CH)
            o_f32 = keep.tile([P, PACK, CH], F32, name=f"o_f32{c}")
            o_il = keep.tile([P, CH, PACK], BF16, name=f"o_il{c}", align_bytes=64)
            if c < NCH - 1:
                nc.scalar.copy(out=o_f32[:], in_=o_ps[c][:])
                nc.sync.dma_start(out=out_rows[:, :, cols], in_=o_f32[:])
            else:
                for u, copy in enumerate((nc.scalar.copy, nc.vector.tensor_copy)):
                    copy(out=o_f32[:, 2 * u : 2 * u + 2, :], in_=last[u][:])
                nc.sync.dma_start(out=out_rows[:, :, cols], in_=o_f32[:])
            interleave(o_copy[c], o_il[:], o_f32[:])
            nc.vector.quantize_mx(out=o_words[:, cols].bitcast(FP8X4), scales=o_scales[:, cols],
                                  in_=o_il[:].rearrange("p c t -> p (c t)"))
            if c >= NCH - 2:
                done = slice(0, (NCH - 1) * CH) if c == NCH - 2 else cols
                nc.sync.dma_start(out=words_hbm[:, done], in_=o_words[:, done].bitcast(I32))
        for q in range(4):
            queue = nc.sync if q % 2 == 0 else nc.scalar
            queue.dma_start(out=scales_hbm[4 * q : 4 * q + 4, :], in_=o_scales[32 * q : 32 * q + 4, :].bitcast(I32))
